import numpy as np
import ml_dtypes

BF16 = ml_dtypes.bfloat16


def bf(x):
    return np.asarray(x, np.float32).astype(BF16)


def f32(x):
    return np.asarray(x, np.float32)


def f64(x):
    return np.asarray(x).astype(np.float64)


def striped(idx):
    return np.tile(idx.reshape(-1, 16).T, (8, 1))


S, K, M, N, E, Q, O = 256, 128, 256, 128, 1, 128, 512


def setup_inputs():
    return {"base": bf(np.random.standard_normal((M, S))), "x": bf(np.random.standard_normal((K, N))), "w": bf(1.2 * np.random.standard_normal((E, K, M)) / np.sqrt(K)), "w2": bf(np.random.standard_normal((M, O)) / np.sqrt(2 * M)), "b": f32(0.5 * np.random.standard_normal((O, 1))), "offs": striped(np.random.permutation(S)[:N])}


def reference(base, x, w, w2, b, offs):
    idx = offs[:16].T.reshape(-1)
    z = f64(base).copy()
    for e in range(E):
        z[:, idx[e * Q : (e + 1) * Q]] += f64(w)[e].T @ f64(x)[:, e * Q : (e + 1) * Q]
    y = f64(w2).T @ z
    return np.maximum(y + f64(b), 0.0)

@@ -1,0 +1,64 @@
+import concourse.mybir as mybir
+from concourse.masks import make_identity
+
+BF16, F32, U16 = mybir.dt.bfloat16, mybir.dt.float32, mybir.dt.uint16
+ADD, MAX = mybir.AluOpType.add, mybir.AluOpType.max
+RELU = mybir.ActivationFunctionType.Relu
+
+P = 128
+S, K, M, N, O = 256, 128, 256, 128, 512
+M_BLOCKS, O_BLOCKS = M // P, O // P
+FLOPS = 2 * K * M * N + 2 * M * O * S
+
+
+def tile_rows_thenproj_relu_kernel(tc, base, x, w, w2, b, offs, out):
+    nc = tc.nc
+    with (
+        tc.tile_pool(name="held", bufs=1) as held,
+        tc.psum_pool(name="psum", bufs=1) as psum,
+    ):
+        base_sb = held.tile([P, M_BLOCKS, S], BF16)
+        w_sb = held.tile([P, M], BF16)
+        x_sb = held.tile([P, N], BF16)
+        offsets = held.tile([P, N // 16], U16)
+        w2_sb = held.tile([P, M_BLOCKS, O], BF16)
+        bias = held.tile([P, O_BLOCKS], F32)
+
+        nc.sync.dma_start(base_sb[:], base.rearrange("(a p) s -> p a s", p=P))
+        nc.sync.dma_start(w_sb[:], w[0, :, :])
+        nc.sync.dma_start(x_sb[:], x)
+        nc.sync.dma_start(offsets[:], offs)
+        nc.scalar.dma_start(w2_sb[:], w2.rearrange("(a p) o -> p a o", p=P))
+        nc.scalar.dma_start(bias[:], b.rearrange("(c p) one -> p (c one)", p=P))
+
+        identity = held.tile([P, P], BF16)
+        make_identity(nc, identity[:])
+
+        windows = [psum.tile([P, S], F32, name=f"window{a}") for a in range(M_BLOCKS)]
+        for a in range(M_BLOCKS):
+            nc.tensor.matmul(windows[a][:], identity[:], base_sb[:, a, :], start=True, stop=False)
+
+        for a in range(M_BLOCKS):
+            nc.tensor.matmul(
+                windows[a][:].indirect(offsets[:]), w_sb[:, a * P : (a + 1) * P], x_sb[:], start=False, stop=True
+            )
+
+        z = [held.tile([P, S], BF16, name=f"z{a}") for a in range(M_BLOCKS)]
+        for a in range(M_BLOCKS):
+            if a % 2 == 0:
+                nc.vector.tensor_copy(z[a][:], windows[a][:])
+            else:
+                nc.scalar.copy(z[a][:], windows[a][:])
+
+        for c in range(O_BLOCKS):
+            y = psum.tile([P, S], F32, name=f"y{c}")
+            for a in range(M_BLOCKS):
+                nc.tensor.matmul(
+                    y[:], w2_sb[:, a, c * P : (c + 1) * P], z[a][:], start=a == 0, stop=a == M_BLOCKS - 1
+                )
+            result = held.tile([P, S], F32, name=f"result{c}")
+            if c % 2 == 0:
+                nc.vector.tensor_scalar(result[:], y[:], bias[:, c : c + 1], 0.0, ADD, MAX)
+            else:
+                nc.scalar.activation(result[:], y[:], RELU, bias=bias[:, c : c + 1])
+            nc.sync.dma_start(out[c * P : (c + 1) * P, :], result[:])

@@ -8,6 +8,7 @@ RELU = mybir.ActivationFunctionType.Relu
 P = 128
 S, K, M, N, O = 256, 128, 256, 128, 512
 M_BLOCKS, O_BLOCKS = M // P, O // P
+WARM_UPS = 4
 FLOPS = 2 * K * M * N + 2 * M * O * S
 
 
@@ -28,8 +29,14 @@ def tile_rows_thenproj_relu_kernel(tc, base, x, w, w2, b, offs, out):
         nc.sync.dma_start(w_sb[:], w[0, :, :])
         nc.sync.dma_start(x_sb[:], x)
         nc.sync.dma_start(offsets[:], offs)
-        nc.scalar.dma_start(w2_sb[:], w2.rearrange("(a p) o -> p a o", p=P))
-        nc.scalar.dma_start(bias[:], b.rearrange("(c p) one -> p (c one)", p=P))
+        nc.sync.dma_start(w2_sb[:], w2.rearrange("(a p) o -> p a o", p=P))
+        nc.sync.dma_start(bias[:], b.rearrange("(c p) one -> p (c one)", p=P))
+
+        zeros = held.tile([P, 512], BF16)
+        nc.vector.memset(zeros[:], 0.0)
+        unread = psum.tile([P, 512], F32)
+        for i in range(WARM_UPS):
+            nc.tensor.matmul(unread[:], zeros[:, 0:P], zeros[:], start=True, stop=True)
 
         identity = held.tile([P, P], BF16)
         make_identity(nc, identity[:])

@@ -8,7 +8,7 @@ RELU = mybir.ActivationFunctionType.Relu
 P = 128
 S, K, M, N, O = 256, 128, 256, 128, 512
 M_BLOCKS, O_BLOCKS = M // P, O // P
-WARM_UPS = 4
+WARM_UPS = 14
 FLOPS = 2 * K * M * N + 2 * M * O * S
 
 
@@ -32,11 +32,11 @@ def tile_rows_thenproj_relu_kernel(tc, base, x, w, w2, b, offs, out):
         nc.sync.dma_start(w2_sb[:], w2.rearrange("(a p) o -> p a o", p=P))
         nc.sync.dma_start(bias[:], b.rearrange("(c p) one -> p (c one)", p=P))
 
-        zeros = held.tile([P, 512], BF16)
+        zeros = held.tile([P, P], BF16)
         nc.vector.memset(zeros[:], 0.0)
-        unread = psum.tile([P, 512], F32)
+        unread = psum.tile([P, P], F32)
         for i in range(WARM_UPS):
-            nc.tensor.matmul(unread[:], zeros[:, 0:P], zeros[:], start=True, stop=True)
+            nc.tensor.matmul(unread[:], zeros[:], zeros[:], start=True, stop=True)
 
         identity = held.tile([P, P], BF16)
         make_identity(nc, identity[:])

@@ -66,6 +66,7 @@ def tile_rows_thenproj_relu_kernel(tc, base, x, w, w2, b, offs, out):
             result = held.tile([P, S], F32, name=f"result{c}")
             if c % 2 == 0:
                 nc.vector.tensor_scalar(result[:], y[:], bias[:, c : c + 1], 0.0, ADD, MAX)
+                nc.sync.dma_start(out[c * P : (c + 1) * P, :], result[:])
             else:
                 nc.scalar.activation(result[:], y[:], RELU, bias=bias[:, c : c + 1])
-            nc.sync.dma_start(out[c * P : (c + 1) * P, :], result[:])
+                nc.scalar.dma_start(out[c * P : (c + 1) * P, :], result[:])

import concourse.mybir as mybir
from concourse.masks import make_identity

BF16, F32, U16 = mybir.dt.bfloat16, mybir.dt.float32, mybir.dt.uint16
ADD, MAX = mybir.AluOpType.add, mybir.AluOpType.max
RELU = mybir.ActivationFunctionType.Relu

P = 128
S, K, M, N, O = 256, 128, 256, 128, 512
M_BLOCKS, O_BLOCKS = M // P, O // P
WARM_UPS = 14
FLOPS = 2 * K * M * N + 2 * M * O * S


def tile_rows_thenproj_relu_kernel(tc, base, x, w, w2, b, offs, out):
    nc = tc.nc
    with (
        tc.tile_pool(name="held", bufs=1) as held,
        tc.psum_pool(name="psum", bufs=1) as psum,
    ):
        base_sb = held.tile([P, M_BLOCKS, S], BF16)
        w_sb = held.tile([P, M], BF16)
        x_sb = held.tile([P, N], BF16)
        offsets = held.tile([P, N // 16], U16)
        w2_sb = held.tile([P, M_BLOCKS, O], BF16)
        bias = held.tile([P, O_BLOCKS], F32)

        nc.sync.dma_start(base_sb[:], base.rearrange("(a p) s -> p a s", p=P))
        nc.sync.dma_start(w_sb[:], w[0, :, :])
        nc.sync.dma_start(x_sb[:], x)
        nc.sync.dma_start(offsets[:], offs)
        nc.sync.dma_start(w2_sb[:], w2.rearrange("(a p) o -> p a o", p=P))
        nc.sync.dma_start(bias[:], b.rearrange("(c p) one -> p (c one)", p=P))

        zeros = held.tile([P, P], BF16)
        nc.vector.memset(zeros[:], 0.0)
        unread = psum.tile([P, P], F32)
        for i in range(WARM_UPS):
            nc.tensor.matmul(unread[:], zeros[:], zeros[:], start=True, stop=True)

        identity = held.tile([P, P], BF16)
        make_identity(nc, identity[:])

        windows = [psum.tile([P, S], F32, name=f"window{a}") for a in range(M_BLOCKS)]
        for a in range(M_BLOCKS):
            nc.tensor.matmul(windows[a][:], identity[:], base_sb[:, a, :], start=True, stop=False)

        for a in range(M_BLOCKS):
            nc.tensor.matmul(
                windows[a][:].indirect(offsets[:]), w_sb[:, a * P : (a + 1) * P], x_sb[:], start=False, stop=True
            )

        z = [held.tile([P, S], BF16, name=f"z{a}") for a in range(M_BLOCKS)]
        for a in range(M_BLOCKS):
            if a % 2 == 0:
                nc.vector.tensor_copy(z[a][:], windows[a][:])
            else:
                nc.scalar.copy(z[a][:], windows[a][:])

        for c in range(O_BLOCKS):
            y = psum.tile([P, S], F32, name=f"y{c}")
            for a in range(M_BLOCKS):
                nc.tensor.matmul(
                    y[:], w2_sb[:, a, c * P : (c + 1) * P], z[a][:], start=a == 0, stop=a == M_BLOCKS - 1
                )
            result = held.tile([P, S], F32, name=f"result{c}")
            if c % 2 == 0:
                nc.vector.tensor_scalar(result[:], y[:], bias[:, c : c + 1], 0.0, ADD, MAX)
                nc.sync.dma_start(out[c * P : (c + 1) * P, :], result[:])
            else:
                nc.scalar.activation(result[:], y[:], RELU, bias=bias[:, c : c + 1])
                nc.scalar.dma_start(out[c * P : (c + 1) * P, :], result[:])
